import numpy as np
import ml_dtypes


def mxq(x, axis, fmt="e4m3"):
    dtype, down = {"e4m3": (ml_dtypes.float8_e4m3fn, 7), "e5m2": (ml_dtypes.float8_e5m2, 14)}[fmt]
    v = np.moveaxis(np.asarray(x, np.float32).astype(ml_dtypes.bfloat16).astype(np.float64), axis, -1)
    blocks = v.reshape(v.shape[:-1] + (-1, 32))
    amax = np.abs(blocks).max(-1, keepdims=True)
    byte = np.maximum(np.where(amax > 0, np.frexp(amax)[1] - 1 + 127, 0) - down, 1)
    scale = np.exp2(byte - 127.0)
    codes = (blocks / scale).astype(np.float32).astype(dtype).astype(np.float64)
    return np.moveaxis((codes * scale).reshape(v.shape), -1, axis)


WIDE = False


def mx_kscale(k):
    if not WIDE:
        return np.ones(k)
    levels = np.array([10, -10, 5, -5, 0])
    if k % 512:
        return np.exp2(np.random.permutation(np.resize(levels, k // 32))).repeat(32)
    a = np.empty((k // 512, 16))
    for p in range(k // 512):
        a[p, :8] = np.random.permutation(np.resize(levels, 8))
        for g in range(8):
            far = levels[np.abs(levels - a[p, g]) >= 10]
            a[p, g + 8] = far[np.random.randint(len(far))]
    return np.exp2(a.ravel()).repeat(32)


def f64(x):
    return np.asarray(x).astype(np.float64)


def striped(idx):
    return np.tile(idx.reshape(-1, 16).T, (8, 1)).astype(np.uint16)


def unstriped(offs):
    return offs[:16].T.reshape(-1).astype(np.int64)


def pack_weight(w):
    k, n = w.shape
    w = f64(np.asarray(w, np.float32).astype(ml_dtypes.bfloat16)).reshape(k // 32, 32, n)
    amax = np.abs(w).max(1)
    byte = np.clip(np.where(amax > 0, np.frexp(amax)[1] - 1 + 127 - 7, 1), 1, 254)
    scaled = (w * np.exp2(127.0 - byte)[:, None, :]).reshape(k, n).astype(np.float32)
    words = np.ascontiguousarray(scaled.reshape(k // 512, 128, 4, n).transpose(0, 1, 3, 2)).astype(ml_dtypes.float8_e4m3fn).view(np.uint8)
    return words, np.ascontiguousarray(byte.astype(np.uint8).reshape(k // 512, 16, n))


def unpack_weight(words, scales):
    g, p, n, _ = words.shape
    vals = np.ascontiguousarray(words).view(ml_dtypes.float8_e4m3fn).astype(np.float64) * np.repeat(np.exp2(scales.astype(np.float64) - 127.0), 8, axis=1)[..., None]
    return vals.transpose(0, 1, 3, 2).reshape(g * 512, n)


def sigmoid(v):
    return 1.0 / (1.0 + np.exp(-np.maximum(v, -700.0)))

def planes(y):
    n, m = y.shape
    v = y.astype(np.float32).astype(ml_dtypes.bfloat16).astype(np.float64).reshape(n // 32, 32, m)
    top = np.abs(v).max(1)
    byte = np.clip(np.where(top > 0, np.frexp(top)[1] - 1 + 127 - 7, 1), 1, 254)
    codes = (v * np.exp2(127.0 - byte)[:, None, :]).reshape(n, m).astype(np.float32).astype(ml_dtypes.float8_e4m3fn).view(np.uint8)
    words = codes.reshape(n // 512, 128, 4, m).transpose(0, 1, 3, 2)
    return np.ascontiguousarray(words), np.ascontiguousarray(byte.astype(np.uint8).reshape(n // 512, 16, m))


K, T, S, N, H, U = 512, 2048, 256, 512, 512, 1024


def setup_inputs():
    n = np.random.standard_normal
    s = mx_kscale(K)[:, None]
    u = mx_kscale(H)
    packed_xT = pack_weight(n((K, T)) * s)
    packed_w1 = pack_weight(n((K, H)) / np.sqrt(K) / s)
    packed_w2 = pack_weight(n((H, N)) / np.sqrt(H) / u[:, None])
    return {
        "x_words": packed_xT[0],
        "x_scales": packed_xT[1],
        "w1_words": packed_w1[0],
        "w1_scales": packed_w1[1],
        "mem": n((H, U)).astype(np.float32),
        "sl": np.random.uniform(1.0, 2.0, (H, 1)).astype(np.float32),
        "th": (0.5 * n((H, 1))).astype(np.float32),
        "gn": (np.random.uniform(0.5, 1.5, (H, 1)) * u[:, None]).astype(np.float32),
        "w2_words": packed_w2[0],
        "w2_scales": packed_w2[1],
        "sl2": np.random.uniform(1.0, 2.0, (N, 1)).astype(np.float32),
        "th2": (0.5 * n((N, 1))).astype(np.float32),
        "offs": striped(np.random.permutation(T)[:S]),
        "n1": striped(np.random.permutation(U)[:S]),
        "n2": striped(np.random.permutation(S)),
        "n3": striped(np.random.permutation(U)),
        "n4": striped(np.random.permutation(U)),
        "n5": striped(np.random.permutation(U)),
    }


def reference(x_words, x_scales, w1_words, w1_scales, mem, sl, th, gn, w2_words, w2_scales, sl2, th2, offs, n1, n2, n3, n4, n5):
    old = f64(mem)[:, unstriped(n1)]
    xq = unpack_weight(x_words, x_scales)[:, unstriped(offs)]
    y = unpack_weight(w1_words, w1_scales).T @ xq
    sg = sigmoid(f64(sl) * (y[:, unstriped(n2)] - f64(th)))
    nw = old + sg * (y - old)
    pg = f64(mem).copy()
    pg[:, unstriped(n1)] = nw
    z = f64(gn) * pg
    h = unpack_weight(w2_words, w2_scales).T @ mxq(z, 0, "e4m3")
    own = sigmoid(f64(sl2) * (h - f64(th2)))
    sg2 = sigmoid(f64(sl2) * (h[:, unstriped(n3)] - f64(th2)))
    out_0 = h[:, unstriped(n4)] * own + h[:, unstriped(n5)] * sg2
    return (out_0,) + planes(out_0)

@@ -1,0 +1,284 @@
+from contextlib import ExitStack
+
+import concourse.mybir as mybir
+
+K, T, S, N, H, U = 512, 2048, 256, 512, 512, 1024
+FLOPS = 2 * K * H * S + 2 * H * N * U
+
+F32 = mybir.dt.float32
+BF16 = mybir.dt.bfloat16
+U32 = mybir.dt.uint32
+I32 = mybir.dt.int32
+U16 = mybir.dt.uint16
+U8 = mybir.dt.uint8
+FP8X4 = mybir.dt.float8_e4m3fn_x4
+MULT = mybir.AluOpType.mult
+ADD = mybir.AluOpType.add
+SUBTRACT = mybir.AluOpType.subtract
+SIGMOID = mybir.ActivationFunctionType.Sigmoid
+COPY = mybir.ActivationFunctionType.Copy
+
+P = 128
+PACK = 4
+HALF = U // 2
+CHUNKS = ((0, 512), (512, 896), (896, 1024))
+
+
+def entries(offsets, lo, hi):
+    return offsets[:, lo // 16 : hi // 16]
+
+
+def tile_picked_layepgemx_none_po_kernel(
+    tc, x_words, x_scales, w1_words, w1_scales, mem, sl, th, gn, w2_words, w2_scales, sl2, th2,
+    offs, n1, n2, n3, n4, n5, out_0, out_1, out_2,
+):
+    nc = tc.nc
+    with ExitStack() as ctx:
+        keep = ctx.enter_context(tc.tile_pool(name="keep", bufs=1))
+        ring = ctx.enter_context(tc.tile_pool(name="ring", bufs=3))
+        psum = ctx.enter_context(tc.psum_pool(name="psum", bufs=8))
+
+        def held(name, shape, dtype):
+            return keep.tile(shape, dtype, name=name, align_bytes=64)
+
+        def load_list(name, src):
+            dst = keep.tile([P, src.shape[1]], U16, name=name)
+            nc.sync.dma_start(dst[:], src)
+            return dst
+
+        def load_words(name, src):
+            dst = held(name, [P, src.shape[2]], U32)
+            nc.sync.dma_start(dst[:].bitcast(I32), src[0].rearrange("p n t -> p (n t)").bitcast(I32))
+            return dst
+
+        def load_scale_rows(queue, dst, src, quadrants=range(4)):
+            for q in quadrants:
+                queue.dma_start(dst[32 * q : 32 * q + 4, :].bitcast(I32), src[0, 4 * q : 4 * q + 4, :].bitcast(I32))
+
+        def load_column(queue, name, src):
+            dst = held(name, [P, PACK], F32)
+            queue.dma_start(dst[:], src.rearrange("(p t) o -> p (t o)", t=PACK))
+            return dst
+
+        def deal(name, src, dtype):
+            dst = held(name, [P, src.shape[1]], dtype)
+            nc.vector.tensor_copy(
+                dst[:].rearrange("p (t m) -> p m t", t=PACK), src[:].rearrange("p (m t) -> p m t", t=PACK)
+            )
+            return dst
+
+        def interleave(engine_copy, dst, src):
+            engine_copy(
+                dst.rearrange("p (c i) t -> p c t i", i=4), src.rearrange("p t (c i) -> p c t i", i=4)
+            )
+
+        x_scale_rows = held("x_scale_rows", [P, T], U8)
+        w1_scale_rows = held("w1_scale_rows", [P, H], U8)
+        w2_scale_rows = held("w2_scale_rows", [P, N], U8)
+        nc.vector.memset(x_scale_rows[:].bitcast(I32), 0)
+        nc.gpsimd.memset(w1_scale_rows[:].bitcast(I32), 0)
+        nc.vector.memset(w2_scale_rows[:].bitcast(I32), 0)
+
+        offs_sb = load_list("offs_sb", offs)
+        n2_sb = load_list("n2_sb", n2)
+        x_codes = load_words("x_codes", x_words)
+        load_scale_rows(nc.sync, x_scale_rows, x_scales)
+        w1_codes = load_words("w1_codes", w1_words)
+        load_scale_rows(nc.sync, w1_scale_rows, w1_scales, (0, 1))
+        load_scale_rows(nc.gpsimd, w1_scale_rows, w1_scales, (2, 3))
+        sl_sb = load_column(nc.gpsimd, "sl_sb", sl)
+        th_sb = load_column(nc.gpsimd, "th_sb", th)
+        mem_rows = mem.rearrange("(p t) w -> p t w", t=PACK)
+        page = [held(f"page{t}", [P, U], F32) for t in range(PACK)]
+        nc.sync.dma_start(page[0][:], mem_rows[:, 0, :])
+        n1_sb = load_list("n1_sb", n1)
+        for t in range(1, PACK):
+            nc.sync.dma_start(page[t][:], mem_rows[:, t, :])
+        gn_sb = load_column(nc.sync, "gn_sb", gn)
+        w2_codes = load_words("w2_codes", w2_words)
+        load_scale_rows(nc.sync, w2_scale_rows, w2_scales)
+        sl2_sb = load_column(nc.sync, "sl2_sb", sl2)
+        th2_sb = load_column(nc.sync, "th2_sb", th2)
+        n4_sb = load_list("n4_sb", n4)
+        n3_sb = load_list("n3_sb", n3)
+        n5_sb = load_list("n5_sb", n5)
+
+        picked_scales = held("picked_scales", [P, S], U8)
+        picked_codes = held("picked_codes", [P, S], U32)
+        nc.vector.tensor_copy(picked_scales[:], x_scale_rows[:].indirect(offs_sb[:]))
+        w1_scales_dealt = deal("w1_scales_dealt", w1_scale_rows, U8)
+        nc.vector.tensor_copy(picked_codes[:], x_codes[:].indirect(offs_sb[:]))
+        w1_dealt = deal("w1_dealt", w1_codes, U32)
+        bias1 = held("bias1", [P, PACK], F32)
+        nc.vector.scalar_tensor_tensor(bias1[:], sl_sb[:], -1.0, th_sb[:], MULT, MULT)
+
+        y_banks = []
+        for t in range(PACK):
+            bank = psum.tile([P, HALF], F32, name="bank")
+            cols = slice(t * P, (t + 1) * P)
+            nc.tensor.matmul_mx(
+                out=bank[:, :S], lhsT=w1_dealt[:, cols].bitcast(FP8X4), lhsT_scale=w1_scales_dealt[:, cols],
+                rhs=picked_codes[:].bitcast(FP8X4), rhs_scale=picked_scales[:], start=True, stop=True,
+            )
+            y_banks.append(bank)
+
+        z_rows = held("z_rows", [P, PACK, U], BF16)
+        fresh = {}
+
+        def gate(t):
+            y = held(f"y{t}", [P, S], F32)
+            gate_t = held(f"gate{t}", [P, S], F32)
+            old = held(f"old{t}", [P, S], F32)
+            if t == 0:
+                nc.vector.tensor_copy(y[:], y_banks[t][:, :S])
+            else:
+                nc.scalar.copy(y[:], y_banks[t][:, :S])
+            for lo in range(0, S, S // 2):
+                nc.scalar.activation(
+                    gate_t[:, lo : lo + S // 2], y[:].indirect(entries(n2_sb, lo, lo + S // 2)), SIGMOID,
+                    bias=bias1[:, t : t + 1], scale=sl_sb[:, t : t + 1],
+                )
+            if t == 0:
+                nc.vector.tensor_copy(old[:], page[t][:].indirect(n1_sb[:]))
+            else:
+                nc.scalar.activation(old[:], page[t][:].indirect(n1_sb[:]), COPY)
+            fresh[t] = (y, gate_t, old)
+
+        def blend(t):
+            y, gate_t, old = fresh[t]
+            diff = held(f"diff{t}", [P, S], F32)
+            step = held(f"step{t}", [P, S], F32)
+            nc.vector.tensor_tensor(diff[:], y[:], old[:], SUBTRACT)
+            nc.vector.tensor_tensor(step[:], diff[:], gate_t[:], MULT)
+            if t % 2 == 0:
+                nc.vector.tensor_tensor(page[t][:].indirect(n1_sb[:]), old[:], step[:], ADD)
+            else:
+                new = held(f"new{t}", [P, S], F32)
+                nc.vector.tensor_tensor(new[:], old[:], step[:], ADD)
+                nc.scalar.activation(page[t][:].indirect(n1_sb[:]), new[:], COPY)
+
+        gate(0)
+        gate(1)
+        blend(0)
+        gate(2)
+        blend(1)
+        gate(3)
+        blend(2)
+        blend(3)
+        w2_scales_dealt = deal("w2_scales_dealt", w2_scale_rows, U8)
+        w2_dealt = deal("w2_dealt", w2_codes, U32)
+        bias2 = held("bias2", [P, PACK], F32)
+        nc.vector.scalar_tensor_tensor(bias2[:], sl2_sb[:], -1.0, th2_sb[:], MULT, MULT)
+        for t in (0, 2, 1, 3):
+            nc.vector.tensor_scalar(z_rows[:, t, :], page[t][:], gn_sb[:, t : t + 1], None, MULT)
+
+        z_grouped = [held(f"z_grouped{h}", [P, HALF, PACK], BF16) for h in range(2)]
+        z_codes = [held(f"z_codes{h}", [P, HALF], U32) for h in range(2)]
+        z_scales = [held(f"z_scales{h}", [P, HALF], U8) for h in range(2)]
+        interleave(nc.vector.tensor_copy, z_grouped[0][:], z_rows[:, :, :HALF])
+        interleave(nc.scalar.copy, z_grouped[1][:], z_rows[:, :, HALF:])
+        for h in range(2):
+            nc.vector.quantize_mx(
+                out=z_codes[h][:].bitcast(FP8X4), scales=z_scales[h][:],
+                in_=z_grouped[h][:].rearrange("p w t -> p (w t)"),
+            )
+
+        h_banks = {}
+        for t, h in ((0, 0), (1, 0), (0, 1), (1, 1), (2, 0), (2, 1), (3, 0), (3, 1)):
+            bank = psum.tile([P, HALF], F32, name="bank")
+            cols = slice(t * P, (t + 1) * P)
+            nc.tensor.matmul_mx(
+                out=bank[:], lhsT=w2_dealt[:, cols].bitcast(FP8X4), lhsT_scale=w2_scales_dealt[:, cols],
+                rhs=z_codes[h][:].bitcast(FP8X4), rhs_scale=z_scales[h][:], start=True, stop=True,
+            )
+            h_banks[t, h] = bank
+
+        hidden = [held(f"hidden{t}", [P, U], F32) for t in range(PACK)]
+        own = {}
+        other = {}
+
+        def evict(engine_copy, t, h):
+            engine_copy(hidden[t][:, h * HALF : (h + 1) * HALF], h_banks[t, h][:])
+
+        def own_gate(t, h):
+            own[t, h] = held(f"own{t}{h}", [P, HALF], F32)
+            nc.scalar.activation(
+                own[t, h][:], h_banks[t, h][:], SIGMOID, bias=bias2[:, t : t + 1], scale=sl2_sb[:, t : t + 1]
+            )
+
+        def other_gate(t, h):
+            other[t, h] = held(f"other{t}{h}", [P, HALF], F32)
+            nc.scalar.activation(
+                other[t, h][:], hidden[t][:].indirect(entries(n3_sb, h * HALF, (h + 1) * HALF)), SIGMOID,
+                bias=bias2[:, t : t + 1], scale=sl2_sb[:, t : t + 1],
+            )
+
+        result = [held(f"result{c}", [P, PACK, hi - lo], F32) for c, (lo, hi) in enumerate(CHUNKS)]
+        result_grouped = [held(f"result_grouped{c}", [P, hi - lo, PACK], BF16) for c, (lo, hi) in enumerate(CHUNKS)]
+        result_codes = [held(f"result_codes{c}", [P, hi - lo], U32) for c, (lo, hi) in enumerate(CHUNKS)]
+        result_scales = held("result_scales", [P, U], U8)
+        out_rows = out_0.rearrange("(p t) w -> p t w", t=PACK)
+        out_words = out_1[0].rearrange("p w t -> p (w t)").bitcast(I32)
+        terms = {}
+
+        def term(which, c, t):
+            lo, hi = CHUNKS[c]
+            h = lo // HALF
+            offsets, gates = ((n4_sb, own), (n5_sb, other))[which]
+            dst = ring.tile([P, HALF], F32, name=f"term{which}")
+            nc.vector.tensor_tensor(
+                dst[:, : hi - lo], hidden[t][:].indirect(entries(offsets, lo, hi)),
+                gates[t, h][:, lo - h * HALF : hi - h * HALF], MULT,
+            )
+            terms[which, c, t] = dst
+
+        def finish(c, t):
+            lo, hi = CHUNKS[c]
+            nc.vector.tensor_tensor(
+                result[c][:, t, :], terms[0, c, t][:, : hi - lo], terms[1, c, t][:, : hi - lo], ADD
+            )
+            nc.sync.dma_start(out_rows[:, t, lo:hi], result[c][:, t, :])
+
+        def group(c):
+            last = c == len(CHUNKS) - 1
+            interleave(nc.vector.tensor_copy if last else nc.scalar.copy, result_grouped[c][:], result[c][:])
+
+        def quantise(c):
+            lo, hi = CHUNKS[c]
+            nc.vector.quantize_mx(
+                out=result_codes[c][:].bitcast(FP8X4), scales=result_scales[:, lo:hi],
+                in_=result_grouped[c][:].rearrange("p w t -> p (w t)"),
+            )
+            nc.sync.dma_start(out_words[:, lo:hi], result_codes[c][:].bitcast(I32))
+
+        evict(nc.scalar.copy, 0, 0)
+        own_gate(0, 0)
+        evict(nc.vector.tensor_copy, 1, 0)
+        evict(nc.scalar.copy, 0, 1)
+        other_gate(0, 0)
+        steps = [(c, t) for c in range(len(CHUNKS)) for t in range(PACK)]
+        for i, (c, t) in enumerate(steps):
+            term(0, c, t)
+            if i > 0:
+                finish(*steps[i - 1])
+            if t == 0 and c > 0:
+                group(c - 1)
+            if t == 3 and c > 0:
+                quantise(c - 1)
+            term(1, c, t)
+            if c == 0 and t < PACK - 1:
+                if t > 0:
+                    evict(nc.scalar.copy, t + 1, 0)
+                evict(nc.scalar.copy, t + 1, 1)
+                own_gate(t + 1, 0)
+                other_gate(t + 1, 0)
+            elif (c == 0 and t == PACK - 1) or (c == 1 and t < PACK - 1):
+                own_gate((t + 1) % PACK, 1)
+                other_gate((t + 1) % PACK, 1)
+        finish(*steps[-1])
+        group(len(CHUNKS) - 1)
+        quantise(len(CHUNKS) - 1)
+        for q in range(4):
+            nc.scalar.dma_start(
+                out_2[0, 4 * q : 4 * q + 4, :].bitcast(I32), result_scales[32 * q : 32 * q + 4, :].bitcast(I32)
+            )

@@ -51,8 +51,8 @@ def tile_picked_layepgemx_none_po_kernel(
             nc.sync.dma_start(dst[:].bitcast(I32), src[0].rearrange("p n t -> p (n t)").bitcast(I32))
             return dst
 
-        def load_scale_rows(queue, dst, src, quadrants=range(4)):
-            for q in quadrants:
+        def load_scale_rows(queue, dst, src):
+            for q in range(4):
                 queue.dma_start(dst[32 * q : 32 * q + 4, :].bitcast(I32), src[0, 4 * q : 4 * q + 4, :].bitcast(I32))
 
         def load_column(queue, name, src):
@@ -60,9 +60,9 @@ def tile_picked_layepgemx_none_po_kernel(
             queue.dma_start(dst[:], src.rearrange("(p t) o -> p (t o)", t=PACK))
             return dst
 
-        def deal(name, src, dtype):
+        def deal(name, src, dtype, engine_copy=nc.vector.tensor_copy):
             dst = held(name, [P, src.shape[1]], dtype)
-            nc.vector.tensor_copy(
+            engine_copy(
                 dst[:].rearrange("p (t m) -> p m t", t=PACK), src[:].rearrange("p (m t) -> p m t", t=PACK)
             )
             return dst
@@ -80,16 +80,15 @@ def tile_picked_layepgemx_none_po_kernel(
         nc.vector.memset(w2_scale_rows[:].bitcast(I32), 0)
 
         offs_sb = load_list("offs_sb", offs)
-        n2_sb = load_list("n2_sb", n2)
         x_codes = load_words("x_codes", x_words)
         load_scale_rows(nc.sync, x_scale_rows, x_scales)
         w1_codes = load_words("w1_codes", w1_words)
-        load_scale_rows(nc.sync, w1_scale_rows, w1_scales, (0, 1))
-        load_scale_rows(nc.gpsimd, w1_scale_rows, w1_scales, (2, 3))
-        sl_sb = load_column(nc.gpsimd, "sl_sb", sl)
-        th_sb = load_column(nc.gpsimd, "th_sb", th)
         mem_rows = mem.rearrange("(p t) w -> p t w", t=PACK)
         page = [held(f"page{t}", [P, U], F32) for t in range(PACK)]
+        load_scale_rows(nc.gpsimd, w1_scale_rows, w1_scales)
+        n2_sb = load_list("n2_sb", n2)
+        sl_sb = load_column(nc.scalar, "sl_sb", sl)
+        th_sb = load_column(nc.scalar, "th_sb", th)
         nc.sync.dma_start(page[0][:], mem_rows[:, 0, :])
         n1_sb = load_list("n1_sb", n1)
         for t in range(1, PACK):
@@ -122,61 +121,69 @@ def tile_picked_layepgemx_none_po_kernel(
             )
             y_banks.append(bank)
 
-        z_rows = held("z_rows", [P, PACK, U], BF16)
-        fresh = {}
+        y = [held(f"y{t}", [P, S], F32) for t in range(PACK)]
+        gate = [held(f"gate{t}", [P, S], F32) for t in range(PACK)]
+        gap = [held(f"gap{t}", [P, S], F32) for t in range(PACK)]
+        pull = [held(f"pull{t}", [P, S], F32) for t in range(PACK)]
+        new = [held(f"new{t}", [P, S], F32) for t in range(PACK)]
 
-        def gate(t):
-            y = held(f"y{t}", [P, S], F32)
-            gate_t = held(f"gate{t}", [P, S], F32)
-            old = held(f"old{t}", [P, S], F32)
-            if t == 0:
-                nc.vector.tensor_copy(y[:], y_banks[t][:, :S])
-            else:
-                nc.scalar.copy(y[:], y_banks[t][:, :S])
+        def fetch_y(t):
+            nc.vector.tensor_copy(y[t][:], y_banks[t][:, :S])
             for lo in range(0, S, S // 2):
                 nc.scalar.activation(
-                    gate_t[:, lo : lo + S // 2], y[:].indirect(entries(n2_sb, lo, lo + S // 2)), SIGMOID,
+                    gate[t][:, lo : lo + S // 2], y[t][:].indirect(entries(n2_sb, lo, lo + S // 2)), SIGMOID,
                     bias=bias1[:, t : t + 1], scale=sl_sb[:, t : t + 1],
                 )
-            if t == 0:
-                nc.vector.tensor_copy(old[:], page[t][:].indirect(n1_sb[:]))
-            else:
-                nc.scalar.activation(old[:], page[t][:].indirect(n1_sb[:]), COPY)
-            fresh[t] = (y, gate_t, old)
 
-        def blend(t):
-            y, gate_t, old = fresh[t]
-            diff = held(f"diff{t}", [P, S], F32)
-            step = held(f"step{t}", [P, S], F32)
-            nc.vector.tensor_tensor(diff[:], y[:], old[:], SUBTRACT)
-            nc.vector.tensor_tensor(step[:], diff[:], gate_t[:], MULT)
-            if t % 2 == 0:
-                nc.vector.tensor_tensor(page[t][:].indirect(n1_sb[:]), old[:], step[:], ADD)
-            else:
-                new = held(f"new{t}", [P, S], F32)
-                nc.vector.tensor_tensor(new[:], old[:], step[:], ADD)
-                nc.scalar.activation(page[t][:].indirect(n1_sb[:]), new[:], COPY)
+        def make_gap(t):
+            nc.vector.tensor_tensor(gap[t][:], page[t][:].indirect(n1_sb[:]), y[t][:], SUBTRACT)
 
-        gate(0)
-        gate(1)
-        blend(0)
-        gate(2)
-        blend(1)
-        gate(3)
-        blend(2)
-        blend(3)
-        w2_scales_dealt = deal("w2_scales_dealt", w2_scale_rows, U8)
-        w2_dealt = deal("w2_dealt", w2_codes, U32)
+        def make_pull(t):
+            nc.vector.scalar_tensor_tensor(pull[t][:], gate[t][:], 1.0, gap[t][:], SUBTRACT, MULT)
+
+        def make_new(t):
+            nc.vector.tensor_tensor(new[t][:], y[t][:], pull[t][:], SUBTRACT)
+
+        def put(t):
+            if t < PACK - 1:
+                nc.scalar.activation(page[t][:].indirect(n1_sb[:]), new[t][:], COPY)
+            else:
+                nc.vector.tensor_copy(page[t][:].indirect(n1_sb[:]), new[t][:])
+
+        fetch_y(0)
+        fetch_y(1)
+        make_gap(0)
+        fetch_y(2)
+        make_pull(0)
+        fetch_y(3)
+        make_new(0)
+        put(0)
+        make_gap(1)
+        make_gap(2)
+        make_pull(1)
+        make_gap(3)
+        make_new(1)
+        put(1)
+        make_pull(2)
+        make_pull(3)
+        make_new(2)
+        put(2)
+        make_new(3)
         bias2 = held("bias2", [P, PACK], F32)
         nc.vector.scalar_tensor_tensor(bias2[:], sl2_sb[:], -1.0, th2_sb[:], MULT, MULT)
-        for t in (0, 2, 1, 3):
+        put(3)
+        z_rows = held("z_rows", [P, PACK, U], BF16)
+        for t in (0, 1, 3):
             nc.vector.tensor_scalar(z_rows[:, t, :], page[t][:], gn_sb[:, t : t + 1], None, MULT)
+        nc.scalar.activation(z_rows[:, 2, :], page[2][:], COPY, scale=gn_sb[:, 2:3])
+        w2_dealt = deal("w2_dealt", w2_codes, U32, nc.scalar.copy)
 
         z_grouped = [held(f"z_grouped{h}", [P, HALF, PACK], BF16) for h in range(2)]
         z_codes = [held(f"z_codes{h}", [P, HALF], U32) for h in range(2)]
         z_scales = [held(f"z_scales{h}", [P, HALF], U8) for h in range(2)]
         interleave(nc.vector.tensor_copy, z_grouped[0][:], z_rows[:, :, :HALF])
         interleave(nc.scalar.copy, z_grouped[1][:], z_rows[:, :, HALF:])
+        w2_scales_dealt = deal("w2_scales_dealt", w2_scale_rows, U8)
         for h in range(2):
             nc.vector.quantize_mx(
                 out=z_codes[h][:].bitcast(FP8X4), scales=z_scales[h][:],
@@ -184,7 +191,7 @@ def tile_picked_layepgemx_none_po_kernel(
             )
 
         h_banks = {}
-        for t, h in ((0, 0), (1, 0), (0, 1), (1, 1), (2, 0), (2, 1), (3, 0), (3, 1)):
+        for t, h in [(t, h) for t in range(PACK) for h in range(2)]:
             bank = psum.tile([P, HALF], F32, name="bank")
             cols = slice(t * P, (t + 1) * P)
             nc.tensor.matmul_mx(
@@ -194,22 +201,22 @@ def tile_picked_layepgemx_none_po_kernel(
             h_banks[t, h] = bank
 
         hidden = [held(f"hidden{t}", [P, U], F32) for t in range(PACK)]
-        own = {}
-        other = {}
+        own = held("own", [P, PACK, U], F32)
+        other = held("other", [P, PACK, U], F32)
 
         def evict(engine_copy, t, h):
             engine_copy(hidden[t][:, h * HALF : (h + 1) * HALF], h_banks[t, h][:])
 
         def own_gate(t, h):
-            own[t, h] = held(f"own{t}{h}", [P, HALF], F32)
             nc.scalar.activation(
-                own[t, h][:], h_banks[t, h][:], SIGMOID, bias=bias2[:, t : t + 1], scale=sl2_sb[:, t : t + 1]
+                own[:, t, h * HALF : (h + 1) * HALF], h_banks[t, h][:], SIGMOID,
+                bias=bias2[:, t : t + 1], scale=sl2_sb[:, t : t + 1],
             )
 
         def other_gate(t, h):
-            other[t, h] = held(f"other{t}{h}", [P, HALF], F32)
             nc.scalar.activation(
-                other[t, h][:], hidden[t][:].indirect(entries(n3_sb, h * HALF, (h + 1) * HALF)), SIGMOID,
+                other[:, t, h * HALF : (h + 1) * HALF],
+                hidden[t][:].indirect(entries(n3_sb, h * HALF, (h + 1) * HALF)), SIGMOID,
                 bias=bias2[:, t : t + 1], scale=sl2_sb[:, t : t + 1],
             )
 
@@ -219,16 +226,15 @@ def tile_picked_layepgemx_none_po_kernel(
         result_scales = held("result_scales", [P, U], U8)
         out_rows = out_0.rearrange("(p t) w -> p t w", t=PACK)
         out_words = out_1[0].rearrange("p w t -> p (w t)").bitcast(I32)
+        looked_up = ((n4_sb, own), (n5_sb, other))
         terms = {}
 
         def term(which, c, t):
             lo, hi = CHUNKS[c]
-            h = lo // HALF
-            offsets, gates = ((n4_sb, own), (n5_sb, other))[which]
+            offsets, gates = looked_up[which]
             dst = ring.tile([P, HALF], F32, name=f"term{which}")
             nc.vector.tensor_tensor(
-                dst[:, : hi - lo], hidden[t][:].indirect(entries(offsets, lo, hi)),
-                gates[t, h][:, lo - h * HALF : hi - h * HALF], MULT,
+                dst[:, : hi - lo], hidden[t][:].indirect(entries(offsets, lo, hi)), gates[:, t, lo:hi], MULT
             )
             terms[which, c, t] = dst
 
@@ -239,9 +245,8 @@ def tile_picked_layepgemx_none_po_kernel(
             )
             nc.sync.dma_start(out_rows[:, t, lo:hi], result[c][:, t, :])
 
-        def group(c):
-            last = c == len(CHUNKS) - 1
-            interleave(nc.vector.tensor_copy if last else nc.scalar.copy, result_grouped[c][:], result[c][:])
+        def group(engine_copy, c):
+            interleave(engine_copy, result_grouped[c][:], result[c][:])
 
         def quantise(c):
             lo, hi = CHUNKS[c]
@@ -253,31 +258,39 @@ def tile_picked_layepgemx_none_po_kernel(
 
         evict(nc.scalar.copy, 0, 0)
         own_gate(0, 0)
-        evict(nc.vector.tensor_copy, 1, 0)
-        evict(nc.scalar.copy, 0, 1)
+        evict(nc.vector.tensor_copy, 0, 1)
         other_gate(0, 0)
-        steps = [(c, t) for c in range(len(CHUNKS)) for t in range(PACK)]
+        steps = [(c, t) for c in range(2) for t in range(PACK)]
         for i, (c, t) in enumerate(steps):
             term(0, c, t)
             if i > 0:
                 finish(*steps[i - 1])
-            if t == 0 and c > 0:
-                group(c - 1)
-            if t == 3 and c > 0:
-                quantise(c - 1)
             term(1, c, t)
-            if c == 0 and t < PACK - 1:
-                if t > 0:
-                    evict(nc.scalar.copy, t + 1, 0)
-                evict(nc.scalar.copy, t + 1, 1)
-                own_gate(t + 1, 0)
-                other_gate(t + 1, 0)
-            elif (c == 0 and t == PACK - 1) or (c == 1 and t < PACK - 1):
-                own_gate((t + 1) % PACK, 1)
-                other_gate((t + 1) % PACK, 1)
+            if i + 1 < len(steps):
+                c_next, t_next = steps[i + 1]
+                if c_next == 0:
+                    evict(nc.scalar.copy, t_next, 0)
+                    evict(nc.scalar.copy, t_next, 1)
+                own_gate(t_next, c_next)
+                other_gate(t_next, c_next)
+
+        lo, hi = CHUNKS[2]
+        fetched = [held(f"fetched{which}", [P, PACK, hi - lo], F32) for which in range(2)]
+        last_terms = [held(f"last_terms{which}", [P, PACK, hi - lo], F32) for which in range(2)]
+        for which, (offsets, gates) in enumerate(looked_up):
+            for t in range(PACK):
+                nc.scalar.activation(fetched[which][:, t, :], hidden[t][:].indirect(entries(offsets, lo, hi)), COPY)
+        group(nc.scalar.copy, 0)
+        nc.vector.tensor_tensor(last_terms[0][:], fetched[0][:], own[:, :, lo:hi], MULT)
         finish(*steps[-1])
-        group(len(CHUNKS) - 1)
-        quantise(len(CHUNKS) - 1)
+        group(nc.scalar.copy, 1)
+        nc.vector.tensor_tensor(last_terms[1][:], fetched[1][:], other[:, :, lo:hi], MULT)
+        quantise(0)
+        nc.vector.tensor_tensor(result[2][:], last_terms[0][:], last_terms[1][:], ADD)
+        nc.sync.dma_start(out_rows[:, :, lo:hi], result[2][:])
+        group(nc.vector.tensor_copy, 2)
+        quantise(1)
+        quantise(2)
         for q in range(4):
             nc.scalar.dma_start(
                 out_2[0, 4 * q : 4 * q + 4, :].bitcast(I32), result_scales[32 * q : 32 * q + 4, :].bitcast(I32)

@@ -21,6 +21,7 @@ COPY = mybir.ActivationFunctionType.Copy
 P = 128
 PACK = 4
 HALF = U // 2
+QUARTER = U // 4
 CHUNKS = ((0, 512), (512, 896), (896, 1024))
 
 
@@ -35,7 +36,6 @@ def tile_picked_layepgemx_none_po_kernel(
     nc = tc.nc
     with ExitStack() as ctx:
         keep = ctx.enter_context(tc.tile_pool(name="keep", bufs=1))
-        ring = ctx.enter_context(tc.tile_pool(name="ring", bufs=3))
         psum = ctx.enter_context(tc.psum_pool(name="psum", bufs=8))
 
         def held(name, shape, dtype):
@@ -75,20 +75,20 @@ def tile_picked_layepgemx_none_po_kernel(
         x_scale_rows = held("x_scale_rows", [P, T], U8)
         w1_scale_rows = held("w1_scale_rows", [P, H], U8)
         w2_scale_rows = held("w2_scale_rows", [P, N], U8)
-        nc.vector.memset(x_scale_rows[:].bitcast(I32), 0)
-        nc.gpsimd.memset(w1_scale_rows[:].bitcast(I32), 0)
+        nc.gpsimd.memset(x_scale_rows[:].bitcast(I32), 0)
+        nc.vector.memset(w1_scale_rows[:].bitcast(I32), 0)
         nc.vector.memset(w2_scale_rows[:].bitcast(I32), 0)
 
-        offs_sb = load_list("offs_sb", offs)
-        x_codes = load_words("x_codes", x_words)
-        load_scale_rows(nc.sync, x_scale_rows, x_scales)
         w1_codes = load_words("w1_codes", w1_words)
+        offs_sb = load_list("offs_sb", offs)
+        n2_sb = load_list("n2_sb", n2)
+        load_scale_rows(nc.sync, x_scale_rows, x_scales)
+        x_codes = load_words("x_codes", x_words)
+        load_scale_rows(nc.sync, w1_scale_rows, w1_scales)
+        sl_sb = load_column(nc.sync, "sl_sb", sl)
         mem_rows = mem.rearrange("(p t) w -> p t w", t=PACK)
         page = [held(f"page{t}", [P, U], F32) for t in range(PACK)]
-        load_scale_rows(nc.gpsimd, w1_scale_rows, w1_scales)
-        n2_sb = load_list("n2_sb", n2)
-        sl_sb = load_column(nc.scalar, "sl_sb", sl)
-        th_sb = load_column(nc.scalar, "th_sb", th)
+        th_sb = load_column(nc.sync, "th_sb", th)
         nc.sync.dma_start(page[0][:], mem_rows[:, 0, :])
         n1_sb = load_list("n1_sb", n1)
         for t in range(1, PACK):
@@ -105,9 +105,12 @@ def tile_picked_layepgemx_none_po_kernel(
         picked_scales = held("picked_scales", [P, S], U8)
         picked_codes = held("picked_codes", [P, S], U32)
         nc.vector.tensor_copy(picked_scales[:], x_scale_rows[:].indirect(offs_sb[:]))
-        w1_scales_dealt = deal("w1_scales_dealt", w1_scale_rows, U8)
-        nc.vector.tensor_copy(picked_codes[:], x_codes[:].indirect(offs_sb[:]))
         w1_dealt = deal("w1_dealt", w1_codes, U32)
+        nc.vector.tensor_copy(picked_codes[:], x_codes[:].indirect(offs_sb[:]))
+        w1_scales_dealt = held("w1_scales_dealt", [P, PACK, P], U8)
+        w1_scale_view = w1_scale_rows[:].rearrange("p (m t) -> p m t", t=PACK)
+        for rows in (slice(0, 1), slice(1, PACK)):
+            nc.vector.tensor_copy(w1_scales_dealt[:, rows, :].rearrange("p t m -> p m t"), w1_scale_view[:, :, rows])
         bias1 = held("bias1", [P, PACK], F32)
         nc.vector.scalar_tensor_tensor(bias1[:], sl_sb[:], -1.0, th_sb[:], MULT, MULT)
 
@@ -116,14 +119,14 @@ def tile_picked_layepgemx_none_po_kernel(
             bank = psum.tile([P, HALF], F32, name="bank")
             cols = slice(t * P, (t + 1) * P)
             nc.tensor.matmul_mx(
-                out=bank[:, :S], lhsT=w1_dealt[:, cols].bitcast(FP8X4), lhsT_scale=w1_scales_dealt[:, cols],
+                out=bank[:, :S], lhsT=w1_dealt[:, cols].bitcast(FP8X4), lhsT_scale=w1_scales_dealt[:, t, :],
                 rhs=picked_codes[:].bitcast(FP8X4), rhs_scale=picked_scales[:], start=True, stop=True,
             )
             y_banks.append(bank)
 
         y = [held(f"y{t}", [P, S], F32) for t in range(PACK)]
         gate = [held(f"gate{t}", [P, S], F32) for t in range(PACK)]
-        gap = [held(f"gap{t}", [P, S], F32) for t in range(PACK)]
+        gap = {}
         pull = [held(f"pull{t}", [P, S], F32) for t in range(PACK)]
         new = [held(f"new{t}", [P, S], F32) for t in range(PACK)]
 
@@ -136,6 +139,7 @@ def tile_picked_layepgemx_none_po_kernel(
                 )
 
         def make_gap(t):
+            gap[t] = held(f"gap{t}" if t < PACK - 1 else "late", [P, S], F32)
             nc.vector.tensor_tensor(gap[t][:], page[t][:].indirect(n1_sb[:]), y[t][:], SUBTRACT)
 
         def make_pull(t):
@@ -150,66 +154,71 @@ def tile_picked_layepgemx_none_po_kernel(
             else:
                 nc.vector.tensor_copy(page[t][:].indirect(n1_sb[:]), new[t][:])
 
-        fetch_y(0)
-        fetch_y(1)
+        for t in range(3):
+            fetch_y(t)
         make_gap(0)
-        fetch_y(2)
-        make_pull(0)
         fetch_y(3)
+        make_pull(0)
+        make_gap(1)
         make_new(0)
         put(0)
-        make_gap(1)
-        make_gap(2)
         make_pull(1)
-        make_gap(3)
+        make_gap(2)
         make_new(1)
         put(1)
+        make_gap(3)
         make_pull(2)
         make_pull(3)
         make_new(2)
         put(2)
-        make_new(3)
         bias2 = held("bias2", [P, PACK], F32)
         nc.vector.scalar_tensor_tensor(bias2[:], sl2_sb[:], -1.0, th2_sb[:], MULT, MULT)
+        make_new(3)
+        w2_dealt = deal("w2_dealt", w2_codes, U32)
         put(3)
-        z_rows = held("z_rows", [P, PACK, U], BF16)
-        for t in (0, 1, 3):
+        z_rows = held("late", [P, PACK, U], BF16)
+        for t in (0, 3):
             nc.vector.tensor_scalar(z_rows[:, t, :], page[t][:], gn_sb[:, t : t + 1], None, MULT)
-        nc.scalar.activation(z_rows[:, 2, :], page[2][:], COPY, scale=gn_sb[:, 2:3])
-        w2_dealt = deal("w2_dealt", w2_codes, U32, nc.scalar.copy)
+        for t in (1, 2):
+            nc.scalar.activation(z_rows[:, t, :], page[t][:], COPY, scale=gn_sb[:, t : t + 1])
 
-        z_grouped = [held(f"z_grouped{h}", [P, HALF, PACK], BF16) for h in range(2)]
-        z_codes = [held(f"z_codes{h}", [P, HALF], U32) for h in range(2)]
-        z_scales = [held(f"z_scales{h}", [P, HALF], U8) for h in range(2)]
-        interleave(nc.vector.tensor_copy, z_grouped[0][:], z_rows[:, :, :HALF])
-        interleave(nc.scalar.copy, z_grouped[1][:], z_rows[:, :, HALF:])
+        pieces = ((0, HALF), (HALF, HALF + QUARTER), (HALF + QUARTER, U))
+        z_grouped = [held(f"z_grouped{lo}", [P, hi - lo, PACK], BF16) for lo, hi in pieces]
+        z_codes = held("z_codes", [P, U], U32)
+        z_scales = held("z_scales", [P, U], U8)
+        for i, (lo, hi) in enumerate(pieces):
+            interleave(nc.vector.tensor_copy if i == 0 else nc.scalar.copy, z_grouped[i][:], z_rows[:, :, lo:hi])
         w2_scales_dealt = deal("w2_scales_dealt", w2_scale_rows, U8)
-        for h in range(2):
+        for i, (lo, hi) in enumerate(pieces):
             nc.vector.quantize_mx(
-                out=z_codes[h][:].bitcast(FP8X4), scales=z_scales[h][:],
-                in_=z_grouped[h][:].rearrange("p w t -> p (w t)"),
+                out=z_codes[:, lo:hi].bitcast(FP8X4), scales=z_scales[:, lo:hi],
+                in_=z_grouped[i][:].rearrange("p w t -> p (w t)"),
             )
 
         h_banks = {}
-        for t, h in [(t, h) for t in range(PACK) for h in range(2)]:
-            bank = psum.tile([P, HALF], F32, name="bank")
-            cols = slice(t * P, (t + 1) * P)
-            nc.tensor.matmul_mx(
-                out=bank[:], lhsT=w2_dealt[:, cols].bitcast(FP8X4), lhsT_scale=w2_scales_dealt[:, cols],
-                rhs=z_codes[h][:].bitcast(FP8X4), rhs_scale=z_scales[h][:], start=True, stop=True,
-            )
-            h_banks[t, h] = bank
+        halves = ((0, HALF), (HALF, U))
+        for t in range(PACK):
+            for lo, hi in pieces if t == 0 else halves:
+                bank = psum.tile([P, HALF], F32, name="bank")
+                cols = slice(t * P, (t + 1) * P)
+                nc.tensor.matmul_mx(
+                    out=bank[:, : hi - lo], lhsT=w2_dealt[:, cols].bitcast(FP8X4),
+                    lhsT_scale=w2_scales_dealt[:, cols], rhs=z_codes[:, lo:hi].bitcast(FP8X4),
+                    rhs_scale=z_scales[:, lo:hi], start=True, stop=True,
+                )
+                h_banks[t, lo] = bank
 
         hidden = [held(f"hidden{t}", [P, U], F32) for t in range(PACK)]
         own = held("own", [P, PACK, U], F32)
         other = held("other", [P, PACK, U], F32)
 
-        def evict(engine_copy, t, h):
-            engine_copy(hidden[t][:, h * HALF : (h + 1) * HALF], h_banks[t, h][:])
+        def evict(engine_copy, t, lo, hi):
+            engine_copy(hidden[t][:, lo:hi], h_banks[t, lo][:, : hi - lo])
 
         def own_gate(t, h):
+            source = h_banks[t, 0][:] if h == 0 else hidden[t][:, HALF:]
             nc.scalar.activation(
-                own[:, t, h * HALF : (h + 1) * HALF], h_banks[t, h][:], SIGMOID,
+                own[:, t, h * HALF : (h + 1) * HALF], source, SIGMOID,
                 bias=bias2[:, t : t + 1], scale=sl2_sb[:, t : t + 1],
             )
 
@@ -227,26 +236,25 @@ def tile_picked_layepgemx_none_po_kernel(
         out_rows = out_0.rearrange("(p t) w -> p t w", t=PACK)
         out_words = out_1[0].rearrange("p w t -> p (w t)").bitcast(I32)
         looked_up = ((n4_sb, own), (n5_sb, other))
-        terms = {}
+        terms = [
+            [held(f"terms{which}{c}", [P, PACK, hi - lo], F32) for c, (lo, hi) in enumerate(CHUNKS)]
+            for which in range(2)
+        ]
 
         def term(which, c, t):
             lo, hi = CHUNKS[c]
             offsets, gates = looked_up[which]
-            dst = ring.tile([P, HALF], F32, name=f"term{which}")
             nc.vector.tensor_tensor(
-                dst[:, : hi - lo], hidden[t][:].indirect(entries(offsets, lo, hi)), gates[:, t, lo:hi], MULT
+                terms[which][c][:, t, :], hidden[t][:].indirect(entries(offsets, lo, hi)), gates[:, t, lo:hi], MULT
             )
-            terms[which, c, t] = dst
 
-        def finish(c, t):
+        def finish(c, rows):
             lo, hi = CHUNKS[c]
-            nc.vector.tensor_tensor(
-                result[c][:, t, :], terms[0, c, t][:, : hi - lo], terms[1, c, t][:, : hi - lo], ADD
-            )
-            nc.sync.dma_start(out_rows[:, t, lo:hi], result[c][:, t, :])
+            nc.vector.tensor_tensor(result[c][:, rows, :], terms[0][c][:, rows, :], terms[1][c][:, rows, :], ADD)
+            nc.sync.dma_start(out_rows[:, rows, lo:hi], result[c][:, rows, :])
 
-        def group(engine_copy, c):
-            interleave(engine_copy, result_grouped[c][:], result[c][:])
+        def group(c):
+            interleave(nc.scalar.copy, result_grouped[c][:], result[c][:])
 
         def quantise(c):
             lo, hi = CHUNKS[c]
@@ -256,42 +264,45 @@ def tile_picked_layepgemx_none_po_kernel(
             )
             nc.sync.dma_start(out_words[:, lo:hi], result_codes[c][:].bitcast(I32))
 
-        evict(nc.scalar.copy, 0, 0)
+        evict(nc.scalar.copy, 0, 0, HALF)
         own_gate(0, 0)
-        evict(nc.vector.tensor_copy, 0, 1)
+        for lo, hi in pieces[1:]:
+            evict(nc.vector.tensor_copy, 0, lo, hi)
         other_gate(0, 0)
         steps = [(c, t) for c in range(2) for t in range(PACK)]
         for i, (c, t) in enumerate(steps):
             term(0, c, t)
-            if i > 0:
-                finish(*steps[i - 1])
+            if i == 0:
+                evict(nc.vector.tensor_copy, 1, HALF, U)
+            elif i % 2 == 0:
+                c_done, t_done = steps[i - 1]
+                finish(c_done, slice(t_done - 1, t_done + 1))
             term(1, c, t)
             if i + 1 < len(steps):
                 c_next, t_next = steps[i + 1]
                 if c_next == 0:
-                    evict(nc.scalar.copy, t_next, 0)
-                    evict(nc.scalar.copy, t_next, 1)
+                    evict(nc.scalar.copy, t_next, 0, HALF)
+                    if t_next > 1:
+                        evict(nc.scalar.copy, t_next, HALF, U)
                 own_gate(t_next, c_next)
                 other_gate(t_next, c_next)
 
         lo, hi = CHUNKS[2]
         fetched = [held(f"fetched{which}", [P, PACK, hi - lo], F32) for which in range(2)]
-        last_terms = [held(f"last_terms{which}", [P, PACK, hi - lo], F32) for which in range(2)]
         for which, (offsets, gates) in enumerate(looked_up):
             for t in range(PACK):
                 nc.scalar.activation(fetched[which][:, t, :], hidden[t][:].indirect(entries(offsets, lo, hi)), COPY)
-        group(nc.scalar.copy, 0)
-        nc.vector.tensor_tensor(last_terms[0][:], fetched[0][:], own[:, :, lo:hi], MULT)
-        finish(*steps[-1])
-        group(nc.scalar.copy, 1)
-        nc.vector.tensor_tensor(last_terms[1][:], fetched[1][:], other[:, :, lo:hi], MULT)
+        group(0)
+        nc.vector.tensor_tensor(terms[0][2][:], fetched[0][:], own[:, :, lo:hi], MULT)
+        finish(1, slice(2, 4))
+        group(1)
+        nc.vector.tensor_tensor(terms[1][2][:], fetched[1][:], other[:, :, lo:hi], MULT)
         quantise(0)
-        nc.vector.tensor_tensor(result[2][:], last_terms[0][:], last_terms[1][:], ADD)
-        nc.sync.dma_start(out_rows[:, :, lo:hi], result[2][:])
-        group(nc.vector.tensor_copy, 2)
+        finish(2, slice(0, PACK))
+        group(2)
         quantise(1)
         quantise(2)
         for q in range(4):
-            nc.scalar.dma_start(
+            (nc.sync if q == 3 else nc.scalar).dma_start(
                 out_2[0, 4 * q : 4 * q + 4, :].bitcast(I32), result_scales[32 * q : 32 * q + 4, :].bitcast(I32)
             )

from contextlib import ExitStack

import concourse.mybir as mybir

K, T, S, N, H, U = 512, 2048, 256, 512, 512, 1024
FLOPS = 2 * K * H * S + 2 * H * N * U

F32 = mybir.dt.float32
BF16 = mybir.dt.bfloat16
U32 = mybir.dt.uint32
I32 = mybir.dt.int32
U16 = mybir.dt.uint16
U8 = mybir.dt.uint8
FP8X4 = mybir.dt.float8_e4m3fn_x4
MULT = mybir.AluOpType.mult
ADD = mybir.AluOpType.add
SUBTRACT = mybir.AluOpType.subtract
SIGMOID = mybir.ActivationFunctionType.Sigmoid
COPY = mybir.ActivationFunctionType.Copy

P = 128
PACK = 4
HALF = U // 2
QUARTER = U // 4
CHUNKS = ((0, 512), (512, 896), (896, 1024))


def entries(offsets, lo, hi):
    return offsets[:, lo // 16 : hi // 16]


def tile_picked_layepgemx_none_po_kernel(
    tc, x_words, x_scales, w1_words, w1_scales, mem, sl, th, gn, w2_words, w2_scales, sl2, th2,
    offs, n1, n2, n3, n4, n5, out_0, out_1, out_2,
):
    nc = tc.nc
    with ExitStack() as ctx:
        keep = ctx.enter_context(tc.tile_pool(name="keep", bufs=1))
        psum = ctx.enter_context(tc.psum_pool(name="psum", bufs=8))

        def held(name, shape, dtype):
            return keep.tile(shape, dtype, name=name, align_bytes=64)

        def load_list(name, src):
            dst = keep.tile([P, src.shape[1]], U16, name=name)
            nc.sync.dma_start(dst[:], src)
            return dst

        def load_words(name, src):
            dst = held(name, [P, src.shape[2]], U32)
            nc.sync.dma_start(dst[:].bitcast(I32), src[0].rearrange("p n t -> p (n t)").bitcast(I32))
            return dst

        def load_scale_rows(queue, dst, src):
            for q in range(4):
                queue.dma_start(dst[32 * q : 32 * q + 4, :].bitcast(I32), src[0, 4 * q : 4 * q + 4, :].bitcast(I32))

        def load_column(queue, name, src):
            dst = held(name, [P, PACK], F32)
            queue.dma_start(dst[:], src.rearrange("(p t) o -> p (t o)", t=PACK))
            return dst

        def deal(name, src, dtype, engine_copy=nc.vector.tensor_copy):
            dst = held(name, [P, src.shape[1]], dtype)
            engine_copy(
                dst[:].rearrange("p (t m) -> p m t", t=PACK), src[:].rearrange("p (m t) -> p m t", t=PACK)
            )
            return dst

        def interleave(engine_copy, dst, src):
            engine_copy(
                dst.rearrange("p (c i) t -> p c t i", i=4), src.rearrange("p t (c i) -> p c t i", i=4)
            )

        x_scale_rows = held("x_scale_rows", [P, T], U8)
        w1_scale_rows = held("w1_scale_rows", [P, H], U8)
        w2_scale_rows = held("w2_scale_rows", [P, N], U8)
        nc.gpsimd.memset(x_scale_rows[:].bitcast(I32), 0)
        nc.vector.memset(w1_scale_rows[:].bitcast(I32), 0)
        nc.vector.memset(w2_scale_rows[:].bitcast(I32), 0)

        w1_codes = load_words("w1_codes", w1_words)
        offs_sb = load_list("offs_sb", offs)
        n2_sb = load_list("n2_sb", n2)
        load_scale_rows(nc.sync, x_scale_rows, x_scales)
        x_codes = load_words("x_codes", x_words)
        load_scale_rows(nc.sync, w1_scale_rows, w1_scales)
        sl_sb = load_column(nc.sync, "sl_sb", sl)
        mem_rows = mem.rearrange("(p t) w -> p t w", t=PACK)
        page = [held(f"page{t}", [P, U], F32) for t in range(PACK)]
        th_sb = load_column(nc.sync, "th_sb", th)
        nc.sync.dma_start(page[0][:], mem_rows[:, 0, :])
        n1_sb = load_list("n1_sb", n1)
        for t in range(1, PACK):
            nc.sync.dma_start(page[t][:], mem_rows[:, t, :])
        gn_sb = load_column(nc.sync, "gn_sb", gn)
        w2_codes = load_words("w2_codes", w2_words)
        load_scale_rows(nc.sync, w2_scale_rows, w2_scales)
        sl2_sb = load_column(nc.sync, "sl2_sb", sl2)
        th2_sb = load_column(nc.sync, "th2_sb", th2)
        n4_sb = load_list("n4_sb", n4)
        n3_sb = load_list("n3_sb", n3)
        n5_sb = load_list("n5_sb", n5)

        picked_scales = held("picked_scales", [P, S], U8)
        picked_codes = held("picked_codes", [P, S], U32)
        nc.vector.tensor_copy(picked_scales[:], x_scale_rows[:].indirect(offs_sb[:]))
        w1_dealt = deal("w1_dealt", w1_codes, U32)
        nc.vector.tensor_copy(picked_codes[:], x_codes[:].indirect(offs_sb[:]))
        w1_scales_dealt = held("w1_scales_dealt", [P, PACK, P], U8)
        w1_scale_view = w1_scale_rows[:].rearrange("p (m t) -> p m t", t=PACK)
        for rows in (slice(0, 1), slice(1, PACK)):
            nc.vector.tensor_copy(w1_scales_dealt[:, rows, :].rearrange("p t m -> p m t"), w1_scale_view[:, :, rows])
        bias1 = held("bias1", [P, PACK], F32)
        nc.vector.scalar_tensor_tensor(bias1[:], sl_sb[:], -1.0, th_sb[:], MULT, MULT)

        y_banks = []
        for t in range(PACK):
            bank = psum.tile([P, HALF], F32, name="bank")
            cols = slice(t * P, (t + 1) * P)
            nc.tensor.matmul_mx(
                out=bank[:, :S], lhsT=w1_dealt[:, cols].bitcast(FP8X4), lhsT_scale=w1_scales_dealt[:, t, :],
                rhs=picked_codes[:].bitcast(FP8X4), rhs_scale=picked_scales[:], start=True, stop=True,
            )
            y_banks.append(bank)

        y = [held(f"y{t}", [P, S], F32) for t in range(PACK)]
        gate = [held(f"gate{t}", [P, S], F32) for t in range(PACK)]
        gap = {}
        pull = [held(f"pull{t}", [P, S], F32) for t in range(PACK)]
        new = [held(f"new{t}", [P, S], F32) for t in range(PACK)]

        def fetch_y(t):
            nc.vector.tensor_copy(y[t][:], y_banks[t][:, :S])
            for lo in range(0, S, S // 2):
                nc.scalar.activation(
                    gate[t][:, lo : lo + S // 2], y[t][:].indirect(entries(n2_sb, lo, lo + S // 2)), SIGMOID,
                    bias=bias1[:, t : t + 1], scale=sl_sb[:, t : t + 1],
                )

        def make_gap(t):
            gap[t] = held(f"gap{t}" if t < PACK - 1 else "late", [P, S], F32)
            nc.vector.tensor_tensor(gap[t][:], page[t][:].indirect(n1_sb[:]), y[t][:], SUBTRACT)

        def make_pull(t):
            nc.vector.scalar_tensor_tensor(pull[t][:], gate[t][:], 1.0, gap[t][:], SUBTRACT, MULT)

        def make_new(t):
            nc.vector.tensor_tensor(new[t][:], y[t][:], pull[t][:], SUBTRACT)

        def put(t):
            if t < PACK - 1:
                nc.scalar.activation(page[t][:].indirect(n1_sb[:]), new[t][:], COPY)
            else:
                nc.vector.tensor_copy(page[t][:].indirect(n1_sb[:]), new[t][:])

        for t in range(3):
            fetch_y(t)
        make_gap(0)
        fetch_y(3)
        make_pull(0)
        make_gap(1)
        make_new(0)
        put(0)
        make_pull(1)
        make_gap(2)
        make_new(1)
        put(1)
        make_gap(3)
        make_pull(2)
        make_pull(3)
        make_new(2)
        put(2)
        bias2 = held("bias2", [P, PACK], F32)
        nc.vector.scalar_tensor_tensor(bias2[:], sl2_sb[:], -1.0, th2_sb[:], MULT, MULT)
        make_new(3)
        w2_dealt = deal("w2_dealt", w2_codes, U32)
        put(3)
        z_rows = held("late", [P, PACK, U], BF16)
        for t in (0, 3):
            nc.vector.tensor_scalar(z_rows[:, t, :], page[t][:], gn_sb[:, t : t + 1], None, MULT)
        for t in (1, 2):
            nc.scalar.activation(z_rows[:, t, :], page[t][:], COPY, scale=gn_sb[:, t : t + 1])

        pieces = ((0, HALF), (HALF, HALF + QUARTER), (HALF + QUARTER, U))
        z_grouped = [held(f"z_grouped{lo}", [P, hi - lo, PACK], BF16) for lo, hi in pieces]
        z_codes = held("z_codes", [P, U], U32)
        z_scales = held("z_scales", [P, U], U8)
        for i, (lo, hi) in enumerate(pieces):
            interleave(nc.vector.tensor_copy if i == 0 else nc.scalar.copy, z_grouped[i][:], z_rows[:, :, lo:hi])
        w2_scales_dealt = deal("w2_scales_dealt", w2_scale_rows, U8)
        for i, (lo, hi) in enumerate(pieces):
            nc.vector.quantize_mx(
                out=z_codes[:, lo:hi].bitcast(FP8X4), scales=z_scales[:, lo:hi],
                in_=z_grouped[i][:].rearrange("p w t -> p (w t)"),
            )

        h_banks = {}
        halves = ((0, HALF), (HALF, U))
        for t in range(PACK):
            for lo, hi in pieces if t == 0 else halves:
                bank = psum.tile([P, HALF], F32, name="bank")
                cols = slice(t * P, (t + 1) * P)
                nc.tensor.matmul_mx(
                    out=bank[:, : hi - lo], lhsT=w2_dealt[:, cols].bitcast(FP8X4),
                    lhsT_scale=w2_scales_dealt[:, cols], rhs=z_codes[:, lo:hi].bitcast(FP8X4),
                    rhs_scale=z_scales[:, lo:hi], start=True, stop=True,
                )
                h_banks[t, lo] = bank

        hidden = [held(f"hidden{t}", [P, U], F32) for t in range(PACK)]
        own = held("own", [P, PACK, U], F32)
        other = held("other", [P, PACK, U], F32)

        def evict(engine_copy, t, lo, hi):
            engine_copy(hidden[t][:, lo:hi], h_banks[t, lo][:, : hi - lo])

        def own_gate(t, h):
            source = h_banks[t, 0][:] if h == 0 else hidden[t][:, HALF:]
            nc.scalar.activation(
                own[:, t, h * HALF : (h + 1) * HALF], source, SIGMOID,
                bias=bias2[:, t : t + 1], scale=sl2_sb[:, t : t + 1],
            )

        def other_gate(t, h):
            nc.scalar.activation(
                other[:, t, h * HALF : (h + 1) * HALF],
                hidden[t][:].indirect(entries(n3_sb, h * HALF, (h + 1) * HALF)), SIGMOID,
                bias=bias2[:, t : t + 1], scale=sl2_sb[:, t : t + 1],
            )

        result = [held(f"result{c}", [P, PACK, hi - lo], F32) for c, (lo, hi) in enumerate(CHUNKS)]
        result_grouped = [held(f"result_grouped{c}", [P, hi - lo, PACK], BF16) for c, (lo, hi) in enumerate(CHUNKS)]
        result_codes = [held(f"result_codes{c}", [P, hi - lo], U32) for c, (lo, hi) in enumerate(CHUNKS)]
        result_scales = held("result_scales", [P, U], U8)
        out_rows = out_0.rearrange("(p t) w -> p t w", t=PACK)
        out_words = out_1[0].rearrange("p w t -> p (w t)").bitcast(I32)
        looked_up = ((n4_sb, own), (n5_sb, other))
        terms = [
            [held(f"terms{which}{c}", [P, PACK, hi - lo], F32) for c, (lo, hi) in enumerate(CHUNKS)]
            for which in range(2)
        ]

        def term(which, c, t):
            lo, hi = CHUNKS[c]
            offsets, gates = looked_up[which]
            nc.vector.tensor_tensor(
                terms[which][c][:, t, :], hidden[t][:].indirect(entries(offsets, lo, hi)), gates[:, t, lo:hi], MULT
            )

        def finish(c, rows):
            lo, hi = CHUNKS[c]
            nc.vector.tensor_tensor(result[c][:, rows, :], terms[0][c][:, rows, :], terms[1][c][:, rows, :], ADD)
            nc.sync.dma_start(out_rows[:, rows, lo:hi], result[c][:, rows, :])

        def group(c):
            interleave(nc.scalar.copy, result_grouped[c][:], result[c][:])

        def quantise(c):
            lo, hi = CHUNKS[c]
            nc.vector.quantize_mx(
                out=result_codes[c][:].bitcast(FP8X4), scales=result_scales[:, lo:hi],
                in_=result_grouped[c][:].rearrange("p w t -> p (w t)"),
            )
            nc.sync.dma_start(out_words[:, lo:hi], result_codes[c][:].bitcast(I32))

        evict(nc.scalar.copy, 0, 0, HALF)
        own_gate(0, 0)
        for lo, hi in pieces[1:]:
            evict(nc.vector.tensor_copy, 0, lo, hi)
        other_gate(0, 0)
        steps = [(c, t) for c in range(2) for t in range(PACK)]
        for i, (c, t) in enumerate(steps):
            term(0, c, t)
            if i == 0:
                evict(nc.vector.tensor_copy, 1, HALF, U)
            elif i % 2 == 0:
                c_done, t_done = steps[i - 1]
                finish(c_done, slice(t_done - 1, t_done + 1))
            term(1, c, t)
            if i + 1 < len(steps):
                c_next, t_next = steps[i + 1]
                if c_next == 0:
                    evict(nc.scalar.copy, t_next, 0, HALF)
                    if t_next > 1:
                        evict(nc.scalar.copy, t_next, HALF, U)
                own_gate(t_next, c_next)
                other_gate(t_next, c_next)

        lo, hi = CHUNKS[2]
        fetched = [held(f"fetched{which}", [P, PACK, hi - lo], F32) for which in range(2)]
        for which, (offsets, gates) in enumerate(looked_up):
            for t in range(PACK):
                nc.scalar.activation(fetched[which][:, t, :], hidden[t][:].indirect(entries(offsets, lo, hi)), COPY)
        group(0)
        nc.vector.tensor_tensor(terms[0][2][:], fetched[0][:], own[:, :, lo:hi], MULT)
        finish(1, slice(2, 4))
        group(1)
        nc.vector.tensor_tensor(terms[1][2][:], fetched[1][:], other[:, :, lo:hi], MULT)
        quantise(0)
        finish(2, slice(0, PACK))
        group(2)
        quantise(1)
        quantise(2)
        for q in range(4):
            (nc.sync if q == 3 else nc.scalar).dma_start(
                out_2[0, 4 * q : 4 * q + 4, :].bitcast(I32), result_scales[32 * q : 32 * q + 4, :].bitcast(I32)
            )
